import numpy as np
import ml_dtypes


def mxq(x, axis, fmt="e4m3"):
    dtype, down = {"e4m3": (ml_dtypes.float8_e4m3fn, 7), "e5m2": (ml_dtypes.float8_e5m2, 14)}[fmt]
    v = np.moveaxis(np.asarray(x, np.float32).astype(ml_dtypes.bfloat16).astype(np.float64), axis, -1)
    blocks = v.reshape(v.shape[:-1] + (-1, 32))
    amax = np.abs(blocks).max(-1, keepdims=True)
    byte = np.maximum(np.where(amax > 0, np.frexp(amax)[1] - 1 + 127, 0) - down, 1)
    scale = np.exp2(byte - 127.0)
    codes = (blocks / scale).astype(np.float32).astype(dtype).astype(np.float64)
    return np.moveaxis((codes * scale).reshape(v.shape), -1, axis)


WIDE = False


def mx_kscale(k):
    if not WIDE:
        return np.ones(k)
    levels = np.array([10, -10, 5, -5, 0])
    if k % 512:
        return np.exp2(np.random.permutation(np.resize(levels, k // 32))).repeat(32)
    a = np.empty((k // 512, 16))
    for p in range(k // 512):
        a[p, :8] = np.random.permutation(np.resize(levels, 8))
        for g in range(8):
            far = levels[np.abs(levels - a[p, g]) >= 10]
            a[p, g + 8] = far[np.random.randint(len(far))]
    return np.exp2(a.ravel()).repeat(32)


def f64(x):
    return np.asarray(x).astype(np.float64)


def striped8(idx):
    return np.asarray(idx).reshape(8, -1, 16).transpose(0, 2, 1).reshape(128, -1).astype(np.uint16)


def unstriped8(offs):
    return offs.reshape(8, 16, -1).transpose(0, 2, 1).reshape(8, -1).astype(np.int64)


def pick8(x, idx, run):
    r = np.arange(len(x))
    return x[r[:, None], idx[r % (8 * run) // run]]


E2M1 = np.array([0.0, 0.5, 1.0, 1.5, 2.0, 3.0, 4.0, 6.0, -0.0, -0.5, -1.0, -1.5, -2.0, -3.0, -4.0, -6.0])


def pack_weight(w, fmt):
    k, n = w.shape
    w = f64(np.asarray(w, np.float32).astype(ml_dtypes.bfloat16)).reshape(k // 32, 32, n)
    amax = np.abs(w).max(1)
    if fmt == "e4m3":
        byte = np.frexp(amax)[1] - 1 + 127 - 7
    else:
        mant, ex = np.frexp(amax / 6.0)
        byte = np.where(mant > 0.5, ex, ex - 1) + 127
    byte = np.clip(np.where(amax > 0, byte, 1), 1, 254)
    scaled = (w * np.exp2(127.0 - byte)[:, None, :]).reshape(k, n).astype(np.float32)
    by_word = np.ascontiguousarray(scaled.reshape(k // 512, 128, 4, n).transpose(0, 1, 3, 2))
    if fmt == "e4m3":
        words = by_word.astype(ml_dtypes.float8_e4m3fn).view(np.uint8)
    else:
        c = by_word.astype(ml_dtypes.float4_e2m1fn).view(np.uint8) & 0xF
        words = (c[..., 0::2] | (c[..., 1::2] << 4)).reshape(k // 512, 128, 2 * n)
    return np.ascontiguousarray(words), np.ascontiguousarray(byte.astype(np.uint8).reshape(k // 512, 16, n))


def unpack_weight(words, scales, fmt):
    g, _, n = scales.shape
    words = np.ascontiguousarray(words).reshape(g, 128, n, -1)
    if fmt == "e4m3":
        vals = words.view(ml_dtypes.float8_e4m3fn).astype(np.float64)
    else:
        nib = np.empty((g, 128, n, 4), np.uint8)
        nib[..., 0::2] = words & 0xF
        nib[..., 1::2] = words >> 4
        vals = E2M1[nib]
    vals = vals * np.repeat(np.exp2(scales.astype(np.float64) - 127.0), 8, axis=1)[..., None]
    return vals.transpose(0, 1, 3, 2).reshape(g * 512, n)


D, T, I, Q, G = 512, 1024, 512, 128, 64


def setup_inputs():
    n = np.random.standard_normal
    idx = np.stack([np.random.permutation(T)[:I] for _ in range(8)])
    idx2 = np.stack([np.random.permutation(T)[:I] for _ in range(8)])
    fd = mx_kscale(D)
    keysp = pack_weight(n((D, T)) / fd[:, None], "e4m3")
    return {
        "query": (n((D, Q)) * 0.9 / np.sqrt(D) * fd[:, None]).astype(np.float32),
        "query2": (n((D, Q)) * 0.9 / np.sqrt(D) * fd[:, None]).astype(np.float32),
        "keys_words": keysp[0],
        "keys_scales": keysp[1],
        "base": (0.3 * n((Q, I))).astype(np.float32),
        "gain2": (np.random.uniform(0.5, 2.0, (Q, 1))).astype(np.float32),
        "offs": striped8(idx),
        "offs2": striped8(idx2),
    }


def reference(query, query2, keys_words, keys_scales, base, gain2, offs, offs2):
    idx = unstriped8(offs)
    idx2 = unstriped8(offs2)
    keysu = unpack_weight(keys_words, keys_scales, "e4m3")
    queryq = mxq(f64(query), 0, "e4m3")
    a = queryq.T @ keysu
    query2q = mxq(f64(query2), 0, "e4m3")
    b = query2q.T @ keysu
    s = pick8(a, idx, 16) * pick8(b, idx2, 16) - pick8(b, idx, 16) * pick8(a, idx2, 16)
    p = np.exp(s)
    pg = p.reshape(Q, G, I // G).sum(axis=2)
    k0 = np.tanh(pg / np.mean(pg, axis=1, keepdims=True)) / pg / 64.0
    kr = np.repeat(k0, I // G, axis=1)
    w = p * kr
    y = np.tanh(w * f64(gain2) * 256.0) + f64(base)
    return y

@@ -1,0 +1,212 @@
+from contextlib import ExitStack
+
+import concourse.mybir as mybir
+
+D, T, SLOTS, Q = 512, 1024, 512, 128
+RUN = 8
+RUNS = SLOTS // RUN
+FLOPS = 2 * 2 * D * Q * T
+
+F32 = mybir.dt.float32
+BF16 = mybir.dt.bfloat16
+I32 = mybir.dt.int32
+U32 = mybir.dt.uint32
+U16 = mybir.dt.uint16
+U8 = mybir.dt.uint8
+FP8X4 = mybir.dt.float8_e4m3fn_x4
+ALU = mybir.AluOpType
+ACT = mybir.ActivationFunctionType
+AXIS = mybir.AxisListType
+
+P = 128
+PACK = 4
+KEY_HALF = T // 2
+PASS_WIDTHS = ((512, 256, 256), (128, 128, 256, 256, 256))
+HALF = SLOTS // 2
+HALF_RUNS = RUNS // 2
+OUT_PIECE = 128
+BIG = 2.0**100
+
+
+def tile_attend_wedge_evenruns_gated_heads_kernel(
+    tc, query, query2, keys_words, keys_scales, base, gain2, offs, offs2, out
+):
+    nc = tc.nc
+    with ExitStack() as ctx:
+        sb = ctx.enter_context(tc.tile_pool(name="sb", bufs=1))
+        ps = ctx.enter_context(tc.psum_pool(name="ps", bufs=1))
+
+        def column(name):
+            return sb.tile([P, 1], F32, name=name)
+
+        key_scales = sb.tile([P, T], U8, name="key_scales", align_bytes=64)
+        nc.vector.memset(key_scales[:].bitcast(U32), 0)
+        raw = []
+        for n, source in enumerate((query, query2)):
+            tile = sb.tile([P, PACK, Q], F32, name=f"raw{n}")
+            nc.sync.dma_start(out=tile[:], in_=source.rearrange("(p t) q -> p t q", t=PACK))
+            raw.append(tile)
+        for quadrant in range(4):
+            nc.sync.dma_start(
+                out=key_scales[32 * quadrant : 32 * quadrant + 4, :].bitcast(I32),
+                in_=keys_scales[0, 4 * quadrant : 4 * quadrant + 4, :].bitcast(I32),
+            )
+        key_bytes = keys_words[0].rearrange("p n t -> p (n t)")
+        key_words = []
+        for h in range(2):
+            tile = sb.tile([P, KEY_HALF], U32, name=f"key_words{h}", align_bytes=64)
+            nc.sync.dma_start(
+                out=tile[:].bitcast(I32),
+                in_=key_bytes[:, PACK * KEY_HALF * h : PACK * KEY_HALF * (h + 1)].bitcast(I32),
+            )
+            key_words.append(tile)
+        list1 = sb.tile([P, SLOTS // 16], U16, name="list1")
+        nc.sync.dma_start(list1[:], offs)
+        list2 = sb.tile([P, SLOTS // 16], U16, name="list2")
+        nc.sync.dma_start(list2[:], offs2)
+        gain = column("gain")
+        nc.sync.dma_start(out=gain[:], in_=gain2)
+        base_sb = sb.tile([P, SLOTS], F32, name="base_sb")
+        nc.sync.dma_start(out=base_sb[:], in_=base)
+
+        q_codes, q_scales = [], []
+        for n in range(2):
+            grouped = sb.tile([P, Q, PACK], BF16, name=f"grouped{n}", align_bytes=64)
+            nc.vector.tensor_copy(out=grouped[:], in_=raw[n][:].rearrange("p t q -> p q t"))
+            codes = sb.tile([P, Q], U32, name=f"q_codes{n}", align_bytes=64)
+            scales = sb.tile([P, Q], U8, name=f"q_scales{n}", align_bytes=64)
+            nc.vector.quantize_mx(
+                out=codes[:].bitcast(FP8X4), scales=scales[:], in_=grouped[:].rearrange("p q t -> p (q t)")
+            )
+            q_codes.append(codes)
+            q_scales.append(scales)
+
+        a = sb.tile([P, T], F32, name="a")
+        b = sb.tile([P, T], F32, name="b")
+        for n, table in enumerate((a, b)):
+            start = 0
+            for j, width in enumerate(PASS_WIDTHS[n]):
+                h, first = divmod(start, KEY_HALF)
+                cols = slice(start, start + width)
+                start = start + width
+                bank = ps.tile([P, width], F32, name=f"bank{n}_{j}")
+                nc.tensor.matmul_mx(
+                    out=bank[:],
+                    lhsT=q_codes[n][:].bitcast(FP8X4),
+                    lhsT_scale=q_scales[n][:],
+                    rhs=key_words[h][:, first : first + width].bitcast(FP8X4),
+                    rhs_scale=key_scales[:, cols],
+                    start=True,
+                    stop=True,
+                )
+                if n == 1 or j == 0:
+                    nc.scalar.activation(table[:, cols], bank[:], ACT.Copy)
+                else:
+                    nc.vector.tensor_copy(out=table[:, cols], in_=bank[:])
+
+        def entries(lists, h):
+            return lists[:, h * HALF // 16 : (h + 1) * HALF // 16]
+
+        def half_tile(name):
+            return sb.tile([P, HALF], F32, name=name)
+
+        def look_up_scalar(name, table, lists, h):
+            tile = half_tile(name)
+            nc.scalar.activation(tile[:], table[:].indirect(entries(lists, h)), ACT.Copy)
+            return tile
+
+        def look_up_vector(name, table, lists, h):
+            tile = half_tile(name)
+            nc.vector.tensor_copy(tile[:], table[:].indirect(entries(lists, h)))
+            return tile
+
+        def look_up_times(name, table, lists, h, other):
+            tile = half_tile(name)
+            nc.vector.tensor_tensor(tile[:], table[:].indirect(entries(lists, h)), other[:], ALU.mult)
+            return tile
+
+        def by_runs(ap):
+            return ap.rearrange("p (g r) -> p g r", r=RUN)
+
+        def along_runs(ap):
+            return ap.unsqueeze(2).to_broadcast([P, ap.shape[1], RUN])
+
+        a1_0 = look_up_vector("a1_0", a, list1, 0)
+        a2_0 = look_up_vector("a2_0", a, list2, 0)
+        a1_1 = look_up_scalar("a1_1", a, list1, 1)
+        a2_1 = look_up_scalar("a2_1", a, list2, 1)
+        b1_1 = look_up_scalar("b1_1", b, list1, 1)
+
+        shifts = sb.tile([P, 2], F32, name="shifts")
+        totals = sb.tile([P, 2], F32, name="totals")
+        p0 = half_tile("p0")
+        p1 = half_tile("p1")
+
+        left0 = look_up_times("left0", b, list2, 0, a1_0)
+        right0 = look_up_times("right0", b, list1, 0, a2_0)
+        left1 = look_up_times("left1", b, list2, 1, a1_1)
+        s0 = half_tile("s0")
+        nc.vector.tensor_tensor(s0[:], left0[:], right0[:], ALU.subtract)
+        right1 = half_tile("right1")
+        nc.vector.tensor_tensor(right1[:], a2_1[:], b1_1[:], ALU.mult)
+        nc.vector.tensor_reduce(shifts[:, 0:1], s0[:], AXIS.X, ALU.max, negate=True)
+        nc.scalar.activation(p0[:], s0[:], ACT.Exp, bias=shifts[:, 0:1], accum_out=totals[:, 0:1])
+        s1 = half_tile("s1")
+        nc.vector.tensor_tensor(s1[:], left1[:], right1[:], ALU.subtract)
+        minus_s1 = half_tile("minus_s1")
+        nc.vector.tensor_scalar(
+            minus_s1[:], s1[:], -1.0, shifts[:, 0:1], ALU.mult, ALU.min, accum_out=shifts[:, 1:2]
+        )
+        carries = sb.tile([P, 2], F32, name="carries")
+        nc.scalar.activation(carries[:], shifts[:], ACT.Exp, bias=shifts[:, 1:2], scale=-1.0)
+        nc.scalar.activation(
+            p1[:], minus_s1[:], ACT.Exp, bias=shifts[:, 1:2], scale=-1.0, accum_out=totals[:, 1:2]
+        )
+        run_sums = sb.tile([P, RUNS], F32, name="run_sums")
+        own_sums0 = sb.tile([P, HALF_RUNS], F32, name="own_sums0")
+        nc.vector.tensor_reduce(own_sums0[:], by_runs(p0[:]), AXIS.X, ALU.add)
+        nc.scalar.activation(run_sums[:, :HALF_RUNS], own_sums0[:], ACT.Copy, scale=carries[:, 0:1])
+        inverse0 = sb.tile([P, HALF_RUNS], F32, name="inverse0")
+        nc.vector.reciprocal(inverse0[:], own_sums0[:])
+        shares = sb.tile([P, 2], F32, name="shares")
+        mean = column("mean")
+        nc.vector.scalar_tensor_tensor(
+            shares[:], totals[:], 1.0 / RUNS, carries[:], ALU.mult, ALU.mult, accum_out=mean[:]
+        )
+        nc.vector.tensor_reduce(run_sums[:, HALF_RUNS:], by_runs(p1[:]), AXIS.X, ALU.add)
+        inverse_mean = column("inverse_mean")
+        nc.vector.reciprocal(inverse_mean[:], mean[:])
+        gate = sb.tile([P, RUNS], F32, name="gate")
+        nc.scalar.activation(gate[:], run_sums[:], ACT.Tanh, scale=inverse_mean[:])
+        inverse1 = sb.tile([P, HALF_RUNS], F32, name="inverse1")
+        nc.vector.reciprocal(inverse1[:], run_sums[:, HALF_RUNS:])
+        within0 = half_tile("within0")
+        nc.vector.scalar_tensor_tensor(
+            by_runs(within0[:]), along_runs(inverse0[:]), BIG, by_runs(p0[:]), ALU.min, ALU.mult
+        )
+
+        piece_runs = OUT_PIECE // RUN
+        factor1 = sb.tile([P, HALF_RUNS], F32, name="factor1")
+        squashed = []
+
+        def weigh(c, values, factors):
+            cols = slice(c % 2 * OUT_PIECE, (c % 2 + 1) * OUT_PIECE)
+            runs = slice(c % 2 * piece_runs, (c % 2 + 1) * piece_runs)
+            z = sb.tile([P, OUT_PIECE], F32, name=f"z{c}")
+            nc.vector.scalar_tensor_tensor(
+                by_runs(z[:]), by_runs(values[:, cols]), gain[:], along_runs(factors[:, runs]), ALU.mult, ALU.mult
+            )
+            y = sb.tile([P, OUT_PIECE], F32, name=f"y{c}")
+            nc.scalar.activation(y[:], z[:], ACT.Tanh, scale=256.0 / RUNS)
+            squashed.append(y)
+
+        weigh(0, within0, gate)
+        nc.vector.scalar_tensor_tensor(factor1[:], inverse1[:], BIG, gate[:, HALF_RUNS:], ALU.min, ALU.mult)
+        weigh(1, within0, gate)
+        weigh(2, p1, factor1)
+        weigh(3, p1, factor1)
+        for c in range(SLOTS // OUT_PIECE):
+            cols = slice(c * OUT_PIECE, (c + 1) * OUT_PIECE)
+            result = sb.tile([P, OUT_PIECE], F32, name=f"result{c}")
+            nc.vector.tensor_tensor(result[:], squashed[c][:], base_sb[:, cols], ALU.add)
+            nc.sync.dma_start(out=out[:, cols], in_=result[:])

@@ -20,7 +20,7 @@ AXIS = mybir.AxisListType
 
 P = 128
 PACK = 4
-KEY_HALF = T // 2
+KEY_SPLIT = 768
 PASS_WIDTHS = ((512, 256, 256), (128, 128, 256, 256, 256))
 HALF = SLOTS // 2
 HALF_RUNS = RUNS // 2
@@ -41,25 +41,31 @@ def tile_attend_wedge_evenruns_gated_heads_kernel(
 
         key_scales = sb.tile([P, T], U8, name="key_scales", align_bytes=64)
         nc.vector.memset(key_scales[:].bitcast(U32), 0)
-        raw = []
-        for n, source in enumerate((query, query2)):
+
+        def load_query(n, source):
             tile = sb.tile([P, PACK, Q], F32, name=f"raw{n}")
             nc.sync.dma_start(out=tile[:], in_=source.rearrange("(p t) q -> p t q", t=PACK))
-            raw.append(tile)
+            return tile
+
+        key_bytes = keys_words[0].rearrange("p n t -> p (n t)")
+
+        def load_keys(first, last):
+            tile = sb.tile([P, last - first], U32, name=f"key_words{first}", align_bytes=64)
+            nc.sync.dma_start(
+                out=tile[:].bitcast(I32),
+                in_=key_bytes[:, PACK * first : PACK * last].bitcast(I32),
+            )
+            return tile
+
+        raw = [load_query(0, query)]
+        key_words = [load_keys(0, KEY_SPLIT)]
         for quadrant in range(4):
             nc.sync.dma_start(
                 out=key_scales[32 * quadrant : 32 * quadrant + 4, :].bitcast(I32),
                 in_=keys_scales[0, 4 * quadrant : 4 * quadrant + 4, :].bitcast(I32),
             )
-        key_bytes = keys_words[0].rearrange("p n t -> p (n t)")
-        key_words = []
-        for h in range(2):
-            tile = sb.tile([P, KEY_HALF], U32, name=f"key_words{h}", align_bytes=64)
-            nc.sync.dma_start(
-                out=tile[:].bitcast(I32),
-                in_=key_bytes[:, PACK * KEY_HALF * h : PACK * KEY_HALF * (h + 1)].bitcast(I32),
-            )
-            key_words.append(tile)
+        raw.append(load_query(1, query2))
+        key_words.append(load_keys(KEY_SPLIT, T))
         list1 = sb.tile([P, SLOTS // 16], U16, name="list1")
         nc.sync.dma_start(list1[:], offs)
         list2 = sb.tile([P, SLOTS // 16], U16, name="list2")
@@ -86,7 +92,7 @@ def tile_attend_wedge_evenruns_gated_heads_kernel(
         for n, table in enumerate((a, b)):
             start = 0
             for j, width in enumerate(PASS_WIDTHS[n]):
-                h, first = divmod(start, KEY_HALF)
+                h, first = divmod(start, KEY_SPLIT)
                 cols = slice(start, start + width)
                 start = start + width
                 bank = ps.tile([P, width], F32, name=f"bank{n}_{j}")
@@ -99,7 +105,7 @@ def tile_attend_wedge_evenruns_gated_heads_kernel(
                     start=True,
                     stop=True,
                 )
-                if n == 1 or j == 0:
+                if n == 1 or j < 2:
                     nc.scalar.activation(table[:, cols], bank[:], ACT.Copy)
                 else:
                     nc.vector.tensor_copy(out=table[:, cols], in_=bank[:])

@@ -21,7 +21,7 @@ AXIS = mybir.AxisListType
 P = 128
 PACK = 4
 KEY_SPLIT = 768
-PASS_WIDTHS = ((512, 256, 256), (128, 128, 256, 256, 256))
+PASS_WIDTHS = ((512, 256, 128, 128), (256, 256, 256, 256))
 HALF = SLOTS // 2
 HALF_RUNS = RUNS // 2
 OUT_PIECE = 128
@@ -184,35 +184,45 @@ def tile_attend_wedge_evenruns_gated_heads_kernel(
         nc.vector.reciprocal(inverse_mean[:], mean[:])
         gate = sb.tile([P, RUNS], F32, name="gate")
         nc.scalar.activation(gate[:], run_sums[:], ACT.Tanh, scale=inverse_mean[:])
+        piece_runs = OUT_PIECE // RUN
+
+        def share_of_run(c):
+            tile = sb.tile([P, OUT_PIECE], F32, name=f"within{c}")
+            nc.vector.scalar_tensor_tensor(
+                by_runs(tile[:]),
+                along_runs(inverse0[:, c * piece_runs : (c + 1) * piece_runs]),
+                BIG,
+                by_runs(p0[:, c * OUT_PIECE : (c + 1) * OUT_PIECE]),
+                ALU.min,
+                ALU.mult,
+            )
+            return tile
+
+        within0 = share_of_run(0)
         inverse1 = sb.tile([P, HALF_RUNS], F32, name="inverse1")
         nc.vector.reciprocal(inverse1[:], run_sums[:, HALF_RUNS:])
-        within0 = half_tile("within0")
-        nc.vector.scalar_tensor_tensor(
-            by_runs(within0[:]), along_runs(inverse0[:]), BIG, by_runs(p0[:]), ALU.min, ALU.mult
-        )
+        within1 = share_of_run(1)
 
-        piece_runs = OUT_PIECE // RUN
         factor1 = sb.tile([P, HALF_RUNS], F32, name="factor1")
         squashed = []
 
         def weigh(c, values, factors):
-            cols = slice(c % 2 * OUT_PIECE, (c % 2 + 1) * OUT_PIECE)
-            runs = slice(c % 2 * piece_runs, (c % 2 + 1) * piece_runs)
             z = sb.tile([P, OUT_PIECE], F32, name=f"z{c}")
             nc.vector.scalar_tensor_tensor(
-                by_runs(z[:]), by_runs(values[:, cols]), gain[:], along_runs(factors[:, runs]), ALU.mult, ALU.mult
+                by_runs(z[:]), by_runs(values), gain[:], along_runs(factors), ALU.mult, ALU.mult
             )
             y = sb.tile([P, OUT_PIECE], F32, name=f"y{c}")
             nc.scalar.activation(y[:], z[:], ACT.Tanh, scale=256.0 / RUNS)
             squashed.append(y)
 
-        weigh(0, within0, gate)
+        weigh(0, within0[:], gate[:, :piece_runs])
         nc.vector.scalar_tensor_tensor(factor1[:], inverse1[:], BIG, gate[:, HALF_RUNS:], ALU.min, ALU.mult)
-        weigh(1, within0, gate)
-        weigh(2, p1, factor1)
-        weigh(3, p1, factor1)
+        weigh(1, within1[:], gate[:, piece_runs:HALF_RUNS])
+        weigh(2, p1[:, :OUT_PIECE], factor1[:, :piece_runs])
+        weigh(3, p1[:, OUT_PIECE:], factor1[:, piece_runs:])
         for c in range(SLOTS // OUT_PIECE):
             cols = slice(c * OUT_PIECE, (c + 1) * OUT_PIECE)
             result = sb.tile([P, OUT_PIECE], F32, name=f"result{c}")
             nc.vector.tensor_tensor(result[:], squashed[c][:], base_sb[:, cols], ALU.add)
-            nc.sync.dma_start(out=out[:, cols], in_=result[:])
+            queue = nc.scalar if c % 2 == 1 else nc.sync
+            queue.dma_start(out=out[:, cols], in_=result[:])

@@ -21,6 +21,7 @@ AXIS = mybir.AxisListType
 P = 128
 PACK = 4
 KEY_SPLIT = 768
+PLANE = 256
 PASS_WIDTHS = ((512, 256, 128, 128), (256, 256, 256, 256))
 HALF = SLOTS // 2
 HALF_RUNS = RUNS // 2
@@ -39,7 +40,7 @@ def tile_attend_wedge_evenruns_gated_heads_kernel(
         def column(name):
             return sb.tile([P, 1], F32, name=name)
 
-        key_scales = sb.tile([P, T], U8, name="key_scales", align_bytes=64)
+        key_scales = sb.tile([P, PLANE], U8, name="key_scales", align_bytes=64)
         nc.vector.memset(key_scales[:].bitcast(U32), 0)
 
         def load_query(n, source):
@@ -61,8 +62,10 @@ def tile_attend_wedge_evenruns_gated_heads_kernel(
         key_words = [load_keys(0, KEY_SPLIT)]
         for quadrant in range(4):
             nc.sync.dma_start(
-                out=key_scales[32 * quadrant : 32 * quadrant + 4, :].bitcast(I32),
-                in_=keys_scales[0, 4 * quadrant : 4 * quadrant + 4, :].bitcast(I32),
+                out=key_scales[32 * quadrant : 32 * quadrant + 16, :].bitcast(I32),
+                in_=keys_scales[0, 4 * quadrant : 4 * quadrant + 4, :]
+                .rearrange("r (j c) -> j r c", c=PLANE)
+                .bitcast(I32),
             )
         raw.append(load_query(1, query2))
         key_words.append(load_keys(KEY_SPLIT, T))
@@ -92,19 +95,22 @@ def tile_attend_wedge_evenruns_gated_heads_kernel(
         for n, table in enumerate((a, b)):
             start = 0
             for j, width in enumerate(PASS_WIDTHS[n]):
-                h, first = divmod(start, KEY_SPLIT)
                 cols = slice(start, start + width)
-                start = start + width
                 bank = ps.tile([P, width], F32, name=f"bank{n}_{j}")
-                nc.tensor.matmul_mx(
-                    out=bank[:],
-                    lhsT=q_codes[n][:].bitcast(FP8X4),
-                    lhsT_scale=q_scales[n][:],
-                    rhs=key_words[h][:, first : first + width].bitcast(FP8X4),
-                    rhs_scale=key_scales[:, cols],
-                    start=True,
-                    stop=True,
-                )
+                step = min(width, PLANE)
+                for token in range(start, start + width, step):
+                    h, word = divmod(token, KEY_SPLIT)
+                    plane, byte = divmod(token, PLANE)
+                    nc.tensor.matmul_mx(
+                        out=bank[:, token - start : token - start + step],
+                        lhsT=q_codes[n][:].bitcast(FP8X4),
+                        lhsT_scale=q_scales[n][:],
+                        rhs=key_words[h][:, word : word + step].bitcast(FP8X4),
+                        rhs_scale=key_scales[4 * plane :, byte : byte + step],
+                        start=True,
+                        stop=True,
+                    )
+                start = start + width
                 if n == 1 or j < 2:
                     nc.scalar.activation(table[:, cols], bank[:], ACT.Copy)
                 else:

from contextlib import ExitStack

import concourse.mybir as mybir

D, T, SLOTS, Q = 512, 1024, 512, 128
RUN = 8
RUNS = SLOTS // RUN
FLOPS = 2 * 2 * D * Q * T

F32 = mybir.dt.float32
BF16 = mybir.dt.bfloat16
I32 = mybir.dt.int32
U32 = mybir.dt.uint32
U16 = mybir.dt.uint16
U8 = mybir.dt.uint8
FP8X4 = mybir.dt.float8_e4m3fn_x4
ALU = mybir.AluOpType
ACT = mybir.ActivationFunctionType
AXIS = mybir.AxisListType

P = 128
PACK = 4
KEY_SPLIT = 768
PLANE = 256
PASS_WIDTHS = ((512, 256, 128, 128), (256, 256, 256, 256))
HALF = SLOTS // 2
HALF_RUNS = RUNS // 2
OUT_PIECE = 128
BIG = 2.0**100


def tile_attend_wedge_evenruns_gated_heads_kernel(
    tc, query, query2, keys_words, keys_scales, base, gain2, offs, offs2, out
):
    nc = tc.nc
    with ExitStack() as ctx:
        sb = ctx.enter_context(tc.tile_pool(name="sb", bufs=1))
        ps = ctx.enter_context(tc.psum_pool(name="ps", bufs=1))

        def column(name):
            return sb.tile([P, 1], F32, name=name)

        key_scales = sb.tile([P, PLANE], U8, name="key_scales", align_bytes=64)
        nc.vector.memset(key_scales[:].bitcast(U32), 0)

        def load_query(n, source):
            tile = sb.tile([P, PACK, Q], F32, name=f"raw{n}")
            nc.sync.dma_start(out=tile[:], in_=source.rearrange("(p t) q -> p t q", t=PACK))
            return tile

        key_bytes = keys_words[0].rearrange("p n t -> p (n t)")

        def load_keys(first, last):
            tile = sb.tile([P, last - first], U32, name=f"key_words{first}", align_bytes=64)
            nc.sync.dma_start(
                out=tile[:].bitcast(I32),
                in_=key_bytes[:, PACK * first : PACK * last].bitcast(I32),
            )
            return tile

        raw = [load_query(0, query)]
        key_words = [load_keys(0, KEY_SPLIT)]
        for quadrant in range(4):
            nc.sync.dma_start(
                out=key_scales[32 * quadrant : 32 * quadrant + 16, :].bitcast(I32),
                in_=keys_scales[0, 4 * quadrant : 4 * quadrant + 4, :]
                .rearrange("r (j c) -> j r c", c=PLANE)
                .bitcast(I32),
            )
        raw.append(load_query(1, query2))
        key_words.append(load_keys(KEY_SPLIT, T))
        list1 = sb.tile([P, SLOTS // 16], U16, name="list1")
        nc.sync.dma_start(list1[:], offs)
        list2 = sb.tile([P, SLOTS // 16], U16, name="list2")
        nc.sync.dma_start(list2[:], offs2)
        gain = column("gain")
        nc.sync.dma_start(out=gain[:], in_=gain2)
        base_sb = sb.tile([P, SLOTS], F32, name="base_sb")
        nc.sync.dma_start(out=base_sb[:], in_=base)

        q_codes, q_scales = [], []
        for n in range(2):
            grouped = sb.tile([P, Q, PACK], BF16, name=f"grouped{n}", align_bytes=64)
            nc.vector.tensor_copy(out=grouped[:], in_=raw[n][:].rearrange("p t q -> p q t"))
            codes = sb.tile([P, Q], U32, name=f"q_codes{n}", align_bytes=64)
            scales = sb.tile([P, Q], U8, name=f"q_scales{n}", align_bytes=64)
            nc.vector.quantize_mx(
                out=codes[:].bitcast(FP8X4), scales=scales[:], in_=grouped[:].rearrange("p q t -> p (q t)")
            )
            q_codes.append(codes)
            q_scales.append(scales)

        a = sb.tile([P, T], F32, name="a")
        b = sb.tile([P, T], F32, name="b")
        for n, table in enumerate((a, b)):
            start = 0
            for j, width in enumerate(PASS_WIDTHS[n]):
                cols = slice(start, start + width)
                bank = ps.tile([P, width], F32, name=f"bank{n}_{j}")
                step = min(width, PLANE)
                for token in range(start, start + width, step):
                    h, word = divmod(token, KEY_SPLIT)
                    plane, byte = divmod(token, PLANE)
                    nc.tensor.matmul_mx(
                        out=bank[:, token - start : token - start + step],
                        lhsT=q_codes[n][:].bitcast(FP8X4),
                        lhsT_scale=q_scales[n][:],
                        rhs=key_words[h][:, word : word + step].bitcast(FP8X4),
                        rhs_scale=key_scales[4 * plane :, byte : byte + step],
                        start=True,
                        stop=True,
                    )
                start = start + width
                if n == 1 or j < 2:
                    nc.scalar.activation(table[:, cols], bank[:], ACT.Copy)
                else:
                    nc.vector.tensor_copy(out=table[:, cols], in_=bank[:])

        def entries(lists, h):
            return lists[:, h * HALF // 16 : (h + 1) * HALF // 16]

        def half_tile(name):
            return sb.tile([P, HALF], F32, name=name)

        def look_up_scalar(name, table, lists, h):
            tile = half_tile(name)
            nc.scalar.activation(tile[:], table[:].indirect(entries(lists, h)), ACT.Copy)
            return tile

        def look_up_vector(name, table, lists, h):
            tile = half_tile(name)
            nc.vector.tensor_copy(tile[:], table[:].indirect(entries(lists, h)))
            return tile

        def look_up_times(name, table, lists, h, other):
            tile = half_tile(name)
            nc.vector.tensor_tensor(tile[:], table[:].indirect(entries(lists, h)), other[:], ALU.mult)
            return tile

        def by_runs(ap):
            return ap.rearrange("p (g r) -> p g r", r=RUN)

        def along_runs(ap):
            return ap.unsqueeze(2).to_broadcast([P, ap.shape[1], RUN])

        a1_0 = look_up_vector("a1_0", a, list1, 0)
        a2_0 = look_up_vector("a2_0", a, list2, 0)
        a1_1 = look_up_scalar("a1_1", a, list1, 1)
        a2_1 = look_up_scalar("a2_1", a, list2, 1)
        b1_1 = look_up_scalar("b1_1", b, list1, 1)

        shifts = sb.tile([P, 2], F32, name="shifts")
        totals = sb.tile([P, 2], F32, name="totals")
        p0 = half_tile("p0")
        p1 = half_tile("p1")

        left0 = look_up_times("left0", b, list2, 0, a1_0)
        right0 = look_up_times("right0", b, list1, 0, a2_0)
        left1 = look_up_times("left1", b, list2, 1, a1_1)
        s0 = half_tile("s0")
        nc.vector.tensor_tensor(s0[:], left0[:], right0[:], ALU.subtract)
        right1 = half_tile("right1")
        nc.vector.tensor_tensor(right1[:], a2_1[:], b1_1[:], ALU.mult)
        nc.vector.tensor_reduce(shifts[:, 0:1], s0[:], AXIS.X, ALU.max, negate=True)
        nc.scalar.activation(p0[:], s0[:], ACT.Exp, bias=shifts[:, 0:1], accum_out=totals[:, 0:1])
        s1 = half_tile("s1")
        nc.vector.tensor_tensor(s1[:], left1[:], right1[:], ALU.subtract)
        minus_s1 = half_tile("minus_s1")
        nc.vector.tensor_scalar(
            minus_s1[:], s1[:], -1.0, shifts[:, 0:1], ALU.mult, ALU.min, accum_out=shifts[:, 1:2]
        )
        carries = sb.tile([P, 2], F32, name="carries")
        nc.scalar.activation(carries[:], shifts[:], ACT.Exp, bias=shifts[:, 1:2], scale=-1.0)
        nc.scalar.activation(
            p1[:], minus_s1[:], ACT.Exp, bias=shifts[:, 1:2], scale=-1.0, accum_out=totals[:, 1:2]
        )
        run_sums = sb.tile([P, RUNS], F32, name="run_sums")
        own_sums0 = sb.tile([P, HALF_RUNS], F32, name="own_sums0")
        nc.vector.tensor_reduce(own_sums0[:], by_runs(p0[:]), AXIS.X, ALU.add)
        nc.scalar.activation(run_sums[:, :HALF_RUNS], own_sums0[:], ACT.Copy, scale=carries[:, 0:1])
        inverse0 = sb.tile([P, HALF_RUNS], F32, name="inverse0")
        nc.vector.reciprocal(inverse0[:], own_sums0[:])
        shares = sb.tile([P, 2], F32, name="shares")
        mean = column("mean")
        nc.vector.scalar_tensor_tensor(
            shares[:], totals[:], 1.0 / RUNS, carries[:], ALU.mult, ALU.mult, accum_out=mean[:]
        )
        nc.vector.tensor_reduce(run_sums[:, HALF_RUNS:], by_runs(p1[:]), AXIS.X, ALU.add)
        inverse_mean = column("inverse_mean")
        nc.vector.reciprocal(inverse_mean[:], mean[:])
        gate = sb.tile([P, RUNS], F32, name="gate")
        nc.scalar.activation(gate[:], run_sums[:], ACT.Tanh, scale=inverse_mean[:])
        piece_runs = OUT_PIECE // RUN

        def share_of_run(c):
            tile = sb.tile([P, OUT_PIECE], F32, name=f"within{c}")
            nc.vector.scalar_tensor_tensor(
                by_runs(tile[:]),
                along_runs(inverse0[:, c * piece_runs : (c + 1) * piece_runs]),
                BIG,
                by_runs(p0[:, c * OUT_PIECE : (c + 1) * OUT_PIECE]),
                ALU.min,
                ALU.mult,
            )
            return tile

        within0 = share_of_run(0)
        inverse1 = sb.tile([P, HALF_RUNS], F32, name="inverse1")
        nc.vector.reciprocal(inverse1[:], run_sums[:, HALF_RUNS:])
        within1 = share_of_run(1)

        factor1 = sb.tile([P, HALF_RUNS], F32, name="factor1")
        squashed = []

        def weigh(c, values, factors):
            z = sb.tile([P, OUT_PIECE], F32, name=f"z{c}")
            nc.vector.scalar_tensor_tensor(
                by_runs(z[:]), by_runs(values), gain[:], along_runs(factors), ALU.mult, ALU.mult
            )
            y = sb.tile([P, OUT_PIECE], F32, name=f"y{c}")
            nc.scalar.activation(y[:], z[:], ACT.Tanh, scale=256.0 / RUNS)
            squashed.append(y)

        weigh(0, within0[:], gate[:, :piece_runs])
        nc.vector.scalar_tensor_tensor(factor1[:], inverse1[:], BIG, gate[:, HALF_RUNS:], ALU.min, ALU.mult)
        weigh(1, within1[:], gate[:, piece_runs:HALF_RUNS])
        weigh(2, p1[:, :OUT_PIECE], factor1[:, :piece_runs])
        weigh(3, p1[:, OUT_PIECE:], factor1[:, piece_runs:])
        for c in range(SLOTS // OUT_PIECE):
            cols = slice(c * OUT_PIECE, (c + 1) * OUT_PIECE)
            result = sb.tile([P, OUT_PIECE], F32, name=f"result{c}")
            nc.vector.tensor_tensor(result[:], squashed[c][:], base_sb[:, cols], ALU.add)
            queue = nc.scalar if c % 2 == 1 else nc.sync
            queue.dma_start(out=out[:, cols], in_=result[:])
